import numpy as np
import ml_dtypes


def mxq(x, axis, fmt="e4m3"):
    dtype, down = {"e4m3": (ml_dtypes.float8_e4m3fn, 7), "e5m2": (ml_dtypes.float8_e5m2, 14)}[fmt]
    v = np.moveaxis(np.asarray(x, np.float32).astype(ml_dtypes.bfloat16).astype(np.float64), axis, -1)
    blocks = v.reshape(v.shape[:-1] + (-1, 32))
    amax = np.abs(blocks).max(-1, keepdims=True)
    byte = np.maximum(np.where(amax > 0, np.frexp(amax)[1] - 1 + 127, 0) - down, 1)
    scale = np.exp2(byte - 127.0)
    codes = (blocks / scale).astype(np.float32).astype(dtype).astype(np.float64)
    return np.moveaxis((codes * scale).reshape(v.shape), -1, axis)


WIDE = False


def mx_kscale(k, group=512):
    if not WIDE:
        return np.ones(k)
    levels = np.array([10, -10, 5, -5, 0])
    if group != 512:
        return np.exp2(np.random.permutation(np.resize(levels, k // group))).repeat(group)
    if k % 512:
        return np.exp2(np.random.permutation(np.resize(levels, k // 32))).repeat(32)
    a = np.empty((k // 512, 16))
    for p in range(k // 512):
        a[p, :8] = np.random.permutation(np.resize(levels, 8))
        for g in range(8):
            far = levels[np.abs(levels - a[p, g]) >= 10]
            a[p, g + 8] = far[np.random.randint(len(far))]
    return np.exp2(a.ravel()).repeat(32)


def f64(x):
    return np.asarray(x).astype(np.float64)


G, D, M, O, N = 2, 256, 256, 256, 512


def sgn(shape):
    return np.random.uniform(0.5, 2.0, shape) * np.where(np.random.standard_normal(shape) < 0, -1.0, 1.0)


def setup_inputs():
    n = np.random.standard_normal
    s_d = mx_kscale(D, 0)
    s_m = mx_kscale(M, 0)
    return {
        "x": (n((G, D, N)) * s_d[:, None]).astype(np.float32),
        "w1": (n((G, D, M)) / np.sqrt(D) / s_d[:, None]).astype(np.float32),
        "w2": (n((G, D, M)) / np.sqrt(D) / s_d[:, None]).astype(np.float32),
        "so": (np.random.uniform(0.3, 1.0, (G, M, 1))).astype(np.float32),
        "hs": (sgn((G, M, 1)) * s_m[:, None]).astype(np.float32),
        "wo2": (n((G, M, O)) / np.sqrt(M) / s_m[:, None]).astype(np.float32),
        "ob": (0.5 * n((G, O, 1))).astype(np.float32),
        "osc": (np.random.uniform(0.5, 2.0, (G, O, 1))).astype(np.float32),
    }


def reference(x, w1, w2, so, hs, wo2, ob, osc):
    w1q = mxq(f64(w1), 1, "e4m3")
    xq = mxq(f64(x), 1, "e4m3")
    z1 = w1q.transpose(0, 2, 1) @ xq
    w2q = mxq(f64(w2), 1, "e4m3")
    z2 = w2q.transpose(0, 2, 1) @ xq
    nm = np.sqrt(np.square(z1) * np.square(z2) + f64(so))
    h = z1 * z2 / nm
    hh = h * f64(hs)
    wo2q = mxq(f64(wo2), 1, "e4m3")
    hhq = mxq(hh, 1, "e4m3")
    y0 = wo2q.transpose(0, 2, 1) @ hhq
    y = np.tanh(y0 + f64(ob)) * f64(osc)
    return y

@@ -1,0 +1,239 @@
+from contextlib import ExitStack
+
+import concourse.mybir as mybir
+
+G, D, M, O, N = 2, 256, 256, 256, 512
+FLOPS = 2 * G * N * (2 * D * M + M * O)
+
+F32 = mybir.dt.float32
+BF16 = mybir.dt.bfloat16
+U32 = mybir.dt.uint32
+U8 = mybir.dt.uint8
+FP8X4 = mybir.dt.float8_e4m3fn_x4
+ACT = mybir.ActivationFunctionType
+ALU = mybir.AluOpType
+
+P = 128
+R = 64
+PACK = 4
+NMM = 128
+CHUNK = 256
+W_SPLIT = 44
+WO_SPLIT = 36
+
+
+def tile_rows_fagree_kernel(tc, x, w1, w2, so, hs, wo2, ob, osc, out):
+    nc = tc.nc
+    with ExitStack() as ctx:
+        sb = ctx.enter_context(tc.tile_pool(name="sb", bufs=1))
+        ps = ctx.enter_context(tc.psum_pool(name="ps", bufs=1))
+        ctx.enter_context(tc.manual_schedule())
+
+        def tile(name, shape, dtype):
+            return sb.tile(shape, dtype, name=name, align_bytes=64)
+
+        banks = [[ps.tile([P, 512], F32, name="bank%d_%d" % (g, b)) for b in range(4)] for g in range(G)]
+
+        x_rows = x.rearrange("g (p j) n -> (g p) j n", j=PACK)
+        x_raw = [tile("x_raw%d" % c, [P, PACK, CHUNK], F32) for c in range(2)]
+        w_raw = {k: tile("raw_" + k, [P, PACK * 256], F32) for k in ("w1", "w2", "wo2")}
+        par = {k: tile("par_" + k, [P, G, 2], F32) for k in ("so", "hs", "ob", "osc")}
+
+        def load_x(c):
+            nc.sync.dma_start(out=x_raw[c][:], in_=x_rows[:, :, c * CHUNK:(c + 1) * CHUNK])
+
+        def load_w(k, w):
+            nc.sync.dma_start(out=w_raw[k][:], in_=w.rearrange("g (p j) m -> (g p) (j m)", j=PACK))
+
+        def load_par(k, v, queue):
+            queue.dma_start(out=par[k][:], in_=v.rearrange("g (q e) o -> q g (e o)", e=2))
+
+        load_par("hs", hs, nc.scalar)
+        load_par("so", so, nc.scalar)
+        load_x(0)
+        load_w("w1", w1)
+        load_w("w2", w2)
+        load_x(1)
+        load_w("wo2", wo2)
+        load_par("ob", ob, nc.sync)
+        load_par("osc", osc, nc.sync)
+
+        warm_in = tile("warm_in", [P, 1], F32)
+        warm_out = tile("warm_out", [P, 1], F32)
+        nc.gpsimd.memset(warm_in[:], 1.0)
+        nc.scalar.activation(out=warm_out[:], in_=warm_in[:], func=ACT.Abs_reciprocal_sqrt)
+
+        def interleave(name, src, width):
+            dst = tile("il_" + name, [P, width * PACK], BF16)
+            nc.vector.tensor_copy(
+                out=dst[:].rearrange("p (c i j) -> p c j i", i=4, j=PACK),
+                in_=src.rearrange("p j (c i) -> p c j i", i=4),
+            )
+            return dst
+
+        w_il = {k: tile("il_" + k, [P, 256 * PACK], BF16) for k in w_raw}
+
+        def deal(k, copy, part):
+            o = w_il[k][:].rearrange("p (e c i j) -> p c j i e", e=2, i=2, j=PACK)
+            s = w_raw[k][:].rearrange("p (j c i e) -> p c j i e", j=PACK, i=2, e=2)
+            copy(out=o[:, part], in_=s[:, part])
+
+        def interleave_words(k):
+            w = pieces[k][2]
+            dst = tile("il_h%d" % k, [P, w * PACK], BF16)
+            nc.vector.tensor_copy(
+                out=dst[:].bitcast(F32).rearrange("p (c i h) -> p c h i", i=2, h=2),
+                in_=hh_rows[k][:].bitcast(F32).rearrange("p (h c i) -> p c h i", i=2, h=2),
+            )
+            return dst
+
+        def quantize(name, src, width):
+            codes = tile("codes_" + name, [P, width], U32)
+            scales = tile("scales_" + name, [P, width], U8)
+            nc.vector.quantize_mx(out=codes[:].bitcast(FP8X4), scales=scales[:], in_=src[:])
+            return codes, scales
+
+        def product(g, bank, wq, xq, width):
+            rows = slice(R * g, R * (g + 1))
+            for e in range(2):
+                wc = slice(128 * e, 128 * (e + 1))
+                for n0 in range(0, width, NMM):
+                    xc = slice(n0, n0 + NMM)
+                    nc.tensor.matmul_mx(
+                        out=bank[:, e * width + n0:e * width + n0 + NMM],
+                        lhsT=wq[0][rows, wc].bitcast(FP8X4), lhsT_scale=wq[1][rows, wc],
+                        rhs=xq[0][rows, xc].bitcast(FP8X4), rhs_scale=xq[1][rows, xc],
+                        start=True, stop=True,
+                    )
+
+        units = [(g, c) for c in range(2) for g in range(G)]
+        z1s = {u: tile("z1s%d%d" % u, [P, 2, CHUNK], F32) for u in units}
+        prod = {u: tile("prod%d%d" % u, [P, 2, CHUNK], F32) for u in units}
+        pieces = [(0, 0, 256), (1, 0, 128), (1, 128, 128)]
+        gk = [(g, k) for g in range(G) for k in range(3)]
+        sq = {(g, k): tile("sq%d%d" % (g, k), [P, 2, pieces[k][2]], F32) for g, k in gk}
+        rs = {(g, k): tile("rs%d%d" % (g, k), [P, 2, pieces[k][2]], F32) for g, k in gk}
+        hh = {(g, k): tile("hh%d%d" % (g, k), [P, 2 * pieces[k][2]], BF16) for g, k in gk}
+        hh_rows = [tile("hh_rows%d" % k, [P, PACK * pieces[k][2]], BF16) for k in range(3)]
+        hs_safe = tile("hs_safe", [P, G, 2], F32)
+        inv_hs = tile("inv_hs", [P, G, 2], F32)
+
+        def invert_hs():
+            nc.vector.scalar_tensor_tensor(out=hs_safe[:], in0=par["hs"][:], scalar=0.0, in1=par["hs"][:],
+                                           op0=ALU.is_equal, op1=ALU.add)
+            nc.vector.reciprocal(out=inv_hs[:], in_=hs_safe[:])
+
+        def copy_z1(g, c):
+            for e in range(2):
+                nc.scalar.activation(out=z1s[g, c][:, e, :], in_=banks[g][2 * c][:, e * CHUNK:(e + 1) * CHUNK],
+                                     func=ACT.Copy, scale=par["hs"][:, g, e:e + 1])
+
+        def mul_z(g, c):
+            nc.vector.tensor_tensor(out=prod[g, c][:].rearrange("p e n -> p (e n)"), in0=banks[g][2 * c + 1][:],
+                                    in1=z1s[g, c][:].rearrange("p e n -> p (e n)"), op=ALU.mult)
+
+        def square_s(g, k):
+            c, n0, w = pieces[k]
+            for e in range(2):
+                nc.scalar.activation(out=sq[g, k][:, e, :], in_=prod[g, c][:, e, n0:n0 + w], func=ACT.Square,
+                                     scale=inv_hs[:, g, e:e + 1])
+
+        def square_v(g, k):
+            c, n0, w = pieces[k]
+            for e in range(2):
+                nc.vector.scalar_tensor_tensor(out=sq[g, k][:, e, :], in0=prod[g, c][:, e, n0:n0 + w],
+                                               scalar=inv_hs[:, g, e:e + 1], in1=prod[g, c][:, e, n0:n0 + w],
+                                               op0=ALU.mult, op1=ALU.mult)
+
+        on_vector = [(1, 0), (0, 2), (1, 2)]
+
+        def root(g, k):
+            for e in range(2):
+                scale = inv_hs[:, g, e:e + 1] if (g, k) in on_vector else 1.0
+                nc.scalar.activation(out=rs[g, k][:, e, :], in_=sq[g, k][:, e, :],
+                                     func=ACT.Abs_reciprocal_sqrt, bias=par["so"][:, g, e:e + 1], scale=scale)
+
+        def agree(g, k):
+            c, n0, w = pieces[k]
+            nc.vector.tensor_tensor(
+                out=hh[g, k][:].rearrange("p (c i e) -> p c e i", i=4, e=2),
+                in0=prod[g, c][:, :, n0:n0 + w].rearrange("p e (c i) -> p c e i", i=4),
+                in1=rs[g, k][:].rearrange("p e (c i) -> p c e i", i=4),
+                op=ALU.mult,
+            )
+            nc.sync.dma_start(
+                out=hh_rows[k][R * g:R * (g + 1)].rearrange("p (h w) -> p h w", h=2),
+                in_=hh[g, k][:],
+            )
+
+        def finish(g, k):
+            c, n0, w = pieces[k]
+            th = tile("th%d%d" % (g, k), [P, 2, w], F32)
+            res = tile("res%d%d" % (g, k), [P, 2, w], F32)
+            for e in range(2):
+                nc.scalar.activation(out=th[:, e, :], in_=banks[g][k][:, e * w:(e + 1) * w], func=ACT.Tanh,
+                                     bias=par["ob"][:, g, e:e + 1])
+            for e in range(2):
+                nc.vector.tensor_scalar(out=res[:, e, :], in0=th[:, e, :], scalar1=par["osc"][:, g, e:e + 1],
+                                        scalar2=None, op0=ALU.mult)
+            col = c * CHUNK + n0
+            nc.sync.dma_start(out=out[g].rearrange("(q e) n -> q e n", e=2)[:, :, col:col + w], in_=res[:])
+
+        first, rest = slice(0, W_SPLIT), slice(W_SPLIT, 64)
+        invert_hs()
+        x0q = quantize("x0", interleave("x0", x_raw[0][:], CHUNK), CHUNK)
+        deal("w1", nc.vector.tensor_copy, first)
+        deal("w1", nc.scalar.copy, rest)
+        w1q = quantize("w1", w_il["w1"], 256)
+        for g in range(G):
+            product(g, banks[g][0], w1q, x0q, CHUNK)
+        deal("w2", nc.vector.tensor_copy, first)
+        deal("w2", nc.scalar.copy, rest)
+        w2q = quantize("w2", w_il["w2"], 256)
+        for g in range(G):
+            product(g, banks[g][1], w2q, x0q, CHUNK)
+        copy_z1(0, 0)
+        copy_z1(1, 0)
+        x1q = quantize("x1", interleave("x1", x_raw[1][:], CHUNK), CHUNK)
+        for g in range(G):
+            product(g, banks[g][2], w1q, x1q, CHUNK)
+        for g in range(G):
+            product(g, banks[g][3], w2q, x1q, CHUNK)
+        deal("wo2", nc.scalar.copy, slice(WO_SPLIT, 64))
+        mul_z(0, 0)
+        mul_z(1, 0)
+        square_s(0, 0)
+        deal("wo2", nc.vector.tensor_copy, slice(0, WO_SPLIT))
+        root(0, 0)
+        square_v(1, 0)
+        copy_z1(0, 1)
+        agree(0, 0)
+        root(1, 0)
+        mul_z(0, 1)
+        copy_z1(1, 1)
+        agree(1, 0)
+        square_s(0, 1)
+        mul_z(1, 1)
+        root(0, 1)
+        square_v(0, 2)
+        square_s(1, 1)
+        agree(0, 1)
+        square_v(1, 2)
+        root(1, 1)
+        woq = quantize("wo2", w_il["wo2"], 256)
+        root(0, 2)
+        agree(1, 1)
+        root(1, 2)
+        h_il = interleave_words(0)
+        agree(0, 2)
+        agree(1, 2)
+        hq = quantize("h0", h_il, 256)
+        for g in range(G):
+            product(g, banks[g][0], woq, hq, 256)
+        for k in (1, 2):
+            hq = quantize("h%d" % k, interleave_words(k), 128)
+            for g in range(G):
+                product(g, banks[g][k], woq, hq, 128)
+        for k in range(3):
+            for g in range(G):
+                finish(g, k)

@@ -48,12 +48,12 @@ def tile_rows_fagree_kernel(tc, x, w1, w2, so, hs, wo2, ob, osc, out):
         def load_par(k, v, queue):
             queue.dma_start(out=par[k][:], in_=v.rearrange("g (q e) o -> q g (e o)", e=2))
 
-        load_par("hs", hs, nc.scalar)
-        load_par("so", so, nc.scalar)
         load_x(0)
         load_w("w1", w1)
         load_w("w2", w2)
+        load_par("hs", hs, nc.sync)
         load_x(1)
+        load_par("so", so, nc.sync)
         load_w("wo2", wo2)
         load_par("ob", ob, nc.sync)
         load_par("osc", osc, nc.sync)
@@ -93,9 +93,10 @@ def tile_rows_fagree_kernel(tc, x, w1, w2, so, hs, wo2, ob, osc, out):
             nc.vector.quantize_mx(out=codes[:].bitcast(FP8X4), scales=scales[:], in_=src[:])
             return codes, scales
 
-        def product(g, bank, wq, xq, width):
+        def product(g, bank_of, wq, xq, width):
             rows = slice(R * g, R * (g + 1))
             for e in range(2):
+                bank = banks[g][bank_of[e]]
                 wc = slice(128 * e, 128 * (e + 1))
                 for n0 in range(0, width, NMM):
                     xc = slice(n0, n0 + NMM)
@@ -118,9 +119,11 @@ def tile_rows_fagree_kernel(tc, x, w1, w2, so, hs, wo2, ob, osc, out):
         hs_safe = tile("hs_safe", [P, G, 2], F32)
         inv_hs = tile("inv_hs", [P, G, 2], F32)
 
-        def invert_hs():
+        def guard_hs():
             nc.vector.scalar_tensor_tensor(out=hs_safe[:], in0=par["hs"][:], scalar=0.0, in1=par["hs"][:],
                                            op0=ALU.is_equal, op1=ALU.add)
+
+        def invert_hs():
             nc.vector.reciprocal(out=inv_hs[:], in_=hs_safe[:])
 
         def copy_z1(g, c):
@@ -131,6 +134,11 @@ def tile_rows_fagree_kernel(tc, x, w1, w2, so, hs, wo2, ob, osc, out):
         def mul_z(g, c):
             nc.vector.tensor_tensor(out=prod[g, c][:].rearrange("p e n -> p (e n)"), in0=banks[g][2 * c + 1][:],
                                     in1=z1s[g, c][:].rearrange("p e n -> p (e n)"), op=ALU.mult)
+
+        def mul_z_split(g):
+            for e in range(2):
+                nc.vector.tensor_tensor(out=prod[g, 0][:, e, :], in0=banks[g][1 + e][:, e * CHUNK:(e + 1) * CHUNK],
+                                        in1=z1s[g, 0][:, e, :], op=ALU.mult)
 
         def square_s(g, k):
             c, n0, w = pieces[k]
@@ -166,13 +174,19 @@ def tile_rows_fagree_kernel(tc, x, w1, w2, so, hs, wo2, ob, osc, out):
                 in_=hh[g, k][:],
             )
 
-        def finish(g, k):
+        th_tiles = {(g, k): tile("th%d%d" % (g, k), [P, 2, pieces[k][2]], F32) for g, k in gk}
+
+        def squash(g, k):
             c, n0, w = pieces[k]
-            th = tile("th%d%d" % (g, k), [P, 2, w], F32)
-            res = tile("res%d%d" % (g, k), [P, 2, w], F32)
+            th = th_tiles[g, k]
             for e in range(2):
                 nc.scalar.activation(out=th[:, e, :], in_=banks[g][k][:, e * w:(e + 1) * w], func=ACT.Tanh,
                                      bias=par["ob"][:, g, e:e + 1])
+
+        def finish(g, k):
+            c, n0, w = pieces[k]
+            th = th_tiles[g, k]
+            res = tile("res%d%d" % (g, k), [P, 2, w], F32)
             for e in range(2):
                 nc.vector.tensor_scalar(out=res[:, e, :], in0=th[:, e, :], scalar1=par["osc"][:, g, e:e + 1],
                                         scalar2=None, op0=ALU.mult)
@@ -180,29 +194,31 @@ def tile_rows_fagree_kernel(tc, x, w1, w2, so, hs, wo2, ob, osc, out):
             nc.sync.dma_start(out=out[g].rearrange("(q e) n -> q e n", e=2)[:, :, col:col + w], in_=res[:])
 
         first, rest = slice(0, W_SPLIT), slice(W_SPLIT, 64)
-        invert_hs()
         x0q = quantize("x0", interleave("x0", x_raw[0][:], CHUNK), CHUNK)
         deal("w1", nc.vector.tensor_copy, first)
         deal("w1", nc.scalar.copy, rest)
         w1q = quantize("w1", w_il["w1"], 256)
         for g in range(G):
-            product(g, banks[g][0], w1q, x0q, CHUNK)
+            product(g, (0, 0), w1q, x0q, CHUNK)
         deal("w2", nc.vector.tensor_copy, first)
         deal("w2", nc.scalar.copy, rest)
         w2q = quantize("w2", w_il["w2"], 256)
         for g in range(G):
-            product(g, banks[g][1], w2q, x0q, CHUNK)
+            product(g, (1, 2), w2q, x0q, CHUNK)
         copy_z1(0, 0)
         copy_z1(1, 0)
-        x1q = quantize("x1", interleave("x1", x_raw[1][:], CHUNK), CHUNK)
+        guard_hs()
+        x1_il = interleave("x1", x_raw[1][:], CHUNK)
+        invert_hs()
+        mul_z_split(0)
+        x1q = quantize("x1", x1_il, CHUNK)
+        mul_z_split(1)
         for g in range(G):
-            product(g, banks[g][2], w1q, x1q, CHUNK)
+            product(g, (2, 2), w1q, x1q, CHUNK)
         for g in range(G):
-            product(g, banks[g][3], w2q, x1q, CHUNK)
-        deal("wo2", nc.scalar.copy, slice(WO_SPLIT, 64))
-        mul_z(0, 0)
-        mul_z(1, 0)
+            product(g, (3, 3), w2q, x1q, CHUNK)
         square_s(0, 0)
+        deal("wo2", nc.scalar.copy, slice(WO_SPLIT, 64))
         deal("wo2", nc.vector.tensor_copy, slice(0, WO_SPLIT))
         root(0, 0)
         square_v(1, 0)
@@ -229,11 +245,17 @@ def tile_rows_fagree_kernel(tc, x, w1, w2, so, hs, wo2, ob, osc, out):
         agree(1, 2)
         hq = quantize("h0", h_il, 256)
         for g in range(G):
-            product(g, banks[g][0], woq, hq, 256)
-        for k in (1, 2):
-            hq = quantize("h%d" % k, interleave_words(k), 128)
-            for g in range(G):
-                product(g, banks[g][k], woq, hq, 128)
+            product(g, (0, 0), woq, hq, 256)
+        hq = quantize("h1", interleave_words(1), 128)
+        for g in range(G):
+            product(g, (1, 1), woq, hq, 128)
+        squash(0, 0)
+        finish(0, 0)
+        hq = quantize("h2", interleave_words(2), 128)
+        for g in range(G):
+            product(g, (2, 2), woq, hq, 128)
         for k in range(3):
             for g in range(G):
-                finish(g, k)
+                if (g, k) != (0, 0):
+                    squash(g, k)
+                    finish(g, k)

@@ -78,12 +78,13 @@ def tile_rows_fagree_kernel(tc, x, w1, w2, so, hs, wo2, ob, osc, out):
             s = w_raw[k][:].rearrange("p (j c i e) -> p c j i e", j=PACK, i=2, e=2)
             copy(out=o[:, part], in_=s[:, part])
 
-        def interleave_words(k):
-            w = pieces[k][2]
-            dst = tile("il_h%d" % k, [P, w * PACK], BF16)
+        def interleave_words(b):
+            k, n0 = [(0, 0), (0, 128), (1, 0), (2, 0)][b]
+            dst = tile("il_h%d" % b, [P, NMM * PACK], BF16)
+            words = hh_rows[k][:].bitcast(F32).rearrange("p (h n) -> p h n", h=2)[:, :, n0:n0 + NMM]
             nc.vector.tensor_copy(
                 out=dst[:].bitcast(F32).rearrange("p (c i h) -> p c h i", i=2, h=2),
-                in_=hh_rows[k][:].bitcast(F32).rearrange("p (h c i) -> p c h i", i=2, h=2),
+                in_=words.rearrange("p h (c i) -> p c h i", i=2),
             )
             return dst
 
@@ -127,18 +128,15 @@ def tile_rows_fagree_kernel(tc, x, w1, w2, so, hs, wo2, ob, osc, out):
             nc.vector.reciprocal(out=inv_hs[:], in_=hs_safe[:])
 
         def copy_z1(g, c):
-            for e in range(2):
-                nc.scalar.activation(out=z1s[g, c][:, e, :], in_=banks[g][2 * c][:, e * CHUNK:(e + 1) * CHUNK],
-                                     func=ACT.Copy, scale=par["hs"][:, g, e:e + 1])
+            nc.scalar.copy(out=z1s[g, c][:].rearrange("p e n -> p (e n)"), in_=banks[g][2 * c][:])
+
+        z2_banks = [(1, 2), (3, 3)]
 
         def mul_z(g, c):
-            nc.vector.tensor_tensor(out=prod[g, c][:].rearrange("p e n -> p (e n)"), in0=banks[g][2 * c + 1][:],
-                                    in1=z1s[g, c][:].rearrange("p e n -> p (e n)"), op=ALU.mult)
-
-        def mul_z_split(g):
             for e in range(2):
-                nc.vector.tensor_tensor(out=prod[g, 0][:, e, :], in0=banks[g][1 + e][:, e * CHUNK:(e + 1) * CHUNK],
-                                        in1=z1s[g, 0][:, e, :], op=ALU.mult)
+                nc.vector.scalar_tensor_tensor(
+                    out=prod[g, c][:, e, :], in0=banks[g][z2_banks[c][e]][:, e * CHUNK:(e + 1) * CHUNK],
+                    scalar=par["hs"][:, g, e:e + 1], in1=z1s[g, c][:, e, :], op0=ALU.mult, op1=ALU.mult)
 
         def square_s(g, k):
             c, n0, w = pieces[k]
@@ -174,24 +172,26 @@ def tile_rows_fagree_kernel(tc, x, w1, w2, so, hs, wo2, ob, osc, out):
                 in_=hh[g, k][:],
             )
 
-        th_tiles = {(g, k): tile("th%d%d" % (g, k), [P, 2, pieces[k][2]], F32) for g, k in gk}
+        th_tiles = {(g, b): tile("th%d%d" % (g, b), [P, 2, NMM], F32) for g in range(G) for b in range(4)}
 
-        def squash(g, k):
-            c, n0, w = pieces[k]
-            th = th_tiles[g, k]
+        def squash(g, b):
             for e in range(2):
-                nc.scalar.activation(out=th[:, e, :], in_=banks[g][k][:, e * w:(e + 1) * w], func=ACT.Tanh,
-                                     bias=par["ob"][:, g, e:e + 1])
+                nc.scalar.activation(out=th_tiles[g, b][:, e, :], in_=banks[g][b][:, e * NMM:(e + 1) * NMM],
+                                     func=ACT.Tanh, bias=par["ob"][:, g, e:e + 1])
 
-        def finish(g, k):
-            c, n0, w = pieces[k]
-            th = th_tiles[g, k]
-            res = tile("res%d%d" % (g, k), [P, 2, w], F32)
+        def finish(g, b):
+            res = tile("res%d%d" % (g, b), [P, 2, NMM], F32)
             for e in range(2):
-                nc.vector.tensor_scalar(out=res[:, e, :], in0=th[:, e, :], scalar1=par["osc"][:, g, e:e + 1],
-                                        scalar2=None, op0=ALU.mult)
-            col = c * CHUNK + n0
-            nc.sync.dma_start(out=out[g].rearrange("(q e) n -> q e n", e=2)[:, :, col:col + w], in_=res[:])
+                nc.vector.tensor_scalar(out=res[:, e, :], in0=th_tiles[g, b][:, e, :],
+                                        scalar1=par["osc"][:, g, e:e + 1], scalar2=None, op0=ALU.mult)
+            nc.sync.dma_start(out=out[g].rearrange("(q e) n -> q e n", e=2)[:, :, b * NMM:(b + 1) * NMM], in_=res[:])
+
+        def second_layer(b, il):
+            hq = quantize("h%d" % b, il, NMM)
+            for g in range(G):
+                product(g, (b, b), woq, hq, NMM)
+            for g in range(G):
+                squash(g, b)
 
         first, rest = slice(0, W_SPLIT), slice(W_SPLIT, 64)
         x0q = quantize("x0", interleave("x0", x_raw[0][:], CHUNK), CHUNK)
@@ -210,12 +210,11 @@ def tile_rows_fagree_kernel(tc, x, w1, w2, so, hs, wo2, ob, osc, out):
         guard_hs()
         x1_il = interleave("x1", x_raw[1][:], CHUNK)
         invert_hs()
-        mul_z_split(0)
+        mul_z(0, 0)
         x1q = quantize("x1", x1_il, CHUNK)
-        mul_z_split(1)
+        mul_z(1, 0)
         for g in range(G):
             product(g, (2, 2), w1q, x1q, CHUNK)
-        for g in range(G):
             product(g, (3, 3), w2q, x1q, CHUNK)
         square_s(0, 0)
         deal("wo2", nc.scalar.copy, slice(WO_SPLIT, 64))
@@ -236,26 +235,20 @@ def tile_rows_fagree_kernel(tc, x, w1, w2, so, hs, wo2, ob, osc, out):
         agree(0, 1)
         square_v(1, 2)
         root(1, 1)
-        woq = quantize("wo2", w_il["wo2"], 256)
         root(0, 2)
         agree(1, 1)
         root(1, 2)
-        h_il = interleave_words(0)
         agree(0, 2)
+        il = interleave_words(0)
         agree(1, 2)
-        hq = quantize("h0", h_il, 256)
-        for g in range(G):
-            product(g, (0, 0), woq, hq, 256)
-        hq = quantize("h1", interleave_words(1), 128)
-        for g in range(G):
-            product(g, (1, 1), woq, hq, 128)
-        squash(0, 0)
-        finish(0, 0)
-        hq = quantize("h2", interleave_words(2), 128)
-        for g in range(G):
-            product(g, (2, 2), woq, hq, 128)
-        for k in range(3):
+        woq = quantize("wo2", w_il["wo2"], 256)
+        second_layer(0, il)
+        second_layer(1, interleave_words(1))
+        for b in (2, 3):
+            il = interleave_words(b)
+            finish(0, b - 2)
+            second_layer(b, il)
+            finish(1, b - 2)
+        for b in (2, 3):
             for g in range(G):
-                if (g, k) != (0, 0):
-                    squash(g, k)
-                    finish(g, k)
+                finish(g, b)

@@ -37,7 +37,15 @@ def tile_rows_fagree_kernel(tc, x, w1, w2, so, hs, wo2, ob, osc, out):
         x_rows = x.rearrange("g (p j) n -> (g p) j n", j=PACK)
         x_raw = [tile("x_raw%d" % c, [P, PACK, CHUNK], F32) for c in range(2)]
         w_raw = {k: tile("raw_" + k, [P, PACK * 256], F32) for k in ("w1", "w2", "wo2")}
-        par = {k: tile("par_" + k, [P, G, 2], F32) for k in ("so", "hs", "ob", "osc")}
+        par_rows = tile("par_rows", [P, P], F32)
+        par_dealt = tile("par_dealt", [P, P], F32)
+        par_cols = tile("par_cols", [P, P], F32)
+        names = ("so", "hs", "ob", "osc")
+        par = {k: par_cols[:].rearrange("p (g e k) -> p k g e", g=G, e=2)[:, i] for i, k in enumerate(names)}
+        warm_in = tile("warm_in", [P, 1], F32)
+        warm_out = tile("warm_out", [P, 1], F32)
+        nc.vector.memset(par_rows[:], 0.0)
+        nc.vector.memset(warm_in[:], 1.0)
 
         def load_x(c):
             nc.sync.dma_start(out=x_raw[c][:], in_=x_rows[:, :, c * CHUNK:(c + 1) * CHUNK])
@@ -45,22 +53,15 @@ def tile_rows_fagree_kernel(tc, x, w1, w2, so, hs, wo2, ob, osc, out):
         def load_w(k, w):
             nc.sync.dma_start(out=w_raw[k][:], in_=w.rearrange("g (p j) m -> (g p) (j m)", j=PACK))
 
-        def load_par(k, v, queue):
-            queue.dma_start(out=par[k][:], in_=v.rearrange("g (q e) o -> q g (e o)", e=2))
-
         load_x(0)
+        for i, v in enumerate((so, hs, ob, osc)):
+            nc.sync.dma_start(out=par_rows[i:P:32, :].rearrange("p (g f) -> p g f", g=G),
+                                in_=v.rearrange("g (s f) o -> s g (f o)", s=4))
         load_w("w1", w1)
         load_w("w2", w2)
-        load_par("hs", hs, nc.sync)
         load_x(1)
-        load_par("so", so, nc.sync)
         load_w("wo2", wo2)
-        load_par("ob", ob, nc.sync)
-        load_par("osc", osc, nc.sync)
 
-        warm_in = tile("warm_in", [P, 1], F32)
-        warm_out = tile("warm_out", [P, 1], F32)
-        nc.gpsimd.memset(warm_in[:], 1.0)
         nc.scalar.activation(out=warm_out[:], in_=warm_in[:], func=ACT.Abs_reciprocal_sqrt)
 
         def interleave(name, src, width):
@@ -121,7 +122,7 @@ def tile_rows_fagree_kernel(tc, x, w1, w2, so, hs, wo2, ob, osc, out):
         inv_hs = tile("inv_hs", [P, G, 2], F32)
 
         def guard_hs():
-            nc.vector.scalar_tensor_tensor(out=hs_safe[:], in0=par["hs"][:], scalar=0.0, in1=par["hs"][:],
+            nc.vector.scalar_tensor_tensor(out=hs_safe[:], in0=par["hs"], scalar=0.0, in1=par["hs"],
                                            op0=ALU.is_equal, op1=ALU.add)
 
         def invert_hs():
@@ -194,22 +195,26 @@ def tile_rows_fagree_kernel(tc, x, w1, w2, so, hs, wo2, ob, osc, out):
                 squash(g, b)
 
         first, rest = slice(0, W_SPLIT), slice(W_SPLIT, 64)
-        x0q = quantize("x0", interleave("x0", x_raw[0][:], CHUNK), CHUNK)
+        x0_il = interleave("x0", x_raw[0][:], CHUNK)
+        nc.vector.tensor_copy(out=par_dealt[:].rearrange("p (g e i) -> p g e i", g=G, e=2),
+                              in_=par_rows[:].rearrange("p (g i e) -> p g e i", g=G, e=2))
+        x0q = quantize("x0", x0_il, CHUNK)
         deal("w1", nc.vector.tensor_copy, first)
         deal("w1", nc.scalar.copy, rest)
+        nc.vector.transpose(out=par_cols[:], in_=par_dealt[:])
         w1q = quantize("w1", w_il["w1"], 256)
         for g in range(G):
             product(g, (0, 0), w1q, x0q, CHUNK)
         deal("w2", nc.vector.tensor_copy, first)
         deal("w2", nc.scalar.copy, rest)
+        guard_hs()
         w2q = quantize("w2", w_il["w2"], 256)
+        invert_hs()
         for g in range(G):
             product(g, (1, 2), w2q, x0q, CHUNK)
         copy_z1(0, 0)
         copy_z1(1, 0)
-        guard_hs()
         x1_il = interleave("x1", x_raw[1][:], CHUNK)
-        invert_hs()
         mul_z(0, 0)
         x1q = quantize("x1", x1_il, CHUNK)
         mul_z(1, 0)

from contextlib import ExitStack

import concourse.mybir as mybir

G, D, M, O, N = 2, 256, 256, 256, 512
FLOPS = 2 * G * N * (2 * D * M + M * O)

F32 = mybir.dt.float32
BF16 = mybir.dt.bfloat16
U32 = mybir.dt.uint32
U8 = mybir.dt.uint8
FP8X4 = mybir.dt.float8_e4m3fn_x4
ACT = mybir.ActivationFunctionType
ALU = mybir.AluOpType

P = 128
R = 64
PACK = 4
NMM = 128
CHUNK = 256
W_SPLIT = 44
WO_SPLIT = 36


def tile_rows_fagree_kernel(tc, x, w1, w2, so, hs, wo2, ob, osc, out):
    nc = tc.nc
    with ExitStack() as ctx:
        sb = ctx.enter_context(tc.tile_pool(name="sb", bufs=1))
        ps = ctx.enter_context(tc.psum_pool(name="ps", bufs=1))
        ctx.enter_context(tc.manual_schedule())

        def tile(name, shape, dtype):
            return sb.tile(shape, dtype, name=name, align_bytes=64)

        banks = [[ps.tile([P, 512], F32, name="bank%d_%d" % (g, b)) for b in range(4)] for g in range(G)]

        x_rows = x.rearrange("g (p j) n -> (g p) j n", j=PACK)
        x_raw = [tile("x_raw%d" % c, [P, PACK, CHUNK], F32) for c in range(2)]
        w_raw = {k: tile("raw_" + k, [P, PACK * 256], F32) for k in ("w1", "w2", "wo2")}
        par_rows = tile("par_rows", [P, P], F32)
        par_dealt = tile("par_dealt", [P, P], F32)
        par_cols = tile("par_cols", [P, P], F32)
        names = ("so", "hs", "ob", "osc")
        par = {k: par_cols[:].rearrange("p (g e k) -> p k g e", g=G, e=2)[:, i] for i, k in enumerate(names)}
        warm_in = tile("warm_in", [P, 1], F32)
        warm_out = tile("warm_out", [P, 1], F32)
        nc.vector.memset(par_rows[:], 0.0)
        nc.vector.memset(warm_in[:], 1.0)

        def load_x(c):
            nc.sync.dma_start(out=x_raw[c][:], in_=x_rows[:, :, c * CHUNK:(c + 1) * CHUNK])

        def load_w(k, w):
            nc.sync.dma_start(out=w_raw[k][:], in_=w.rearrange("g (p j) m -> (g p) (j m)", j=PACK))

        load_x(0)
        for i, v in enumerate((so, hs, ob, osc)):
            nc.sync.dma_start(out=par_rows[i:P:32, :].rearrange("p (g f) -> p g f", g=G),
                                in_=v.rearrange("g (s f) o -> s g (f o)", s=4))
        load_w("w1", w1)
        load_w("w2", w2)
        load_x(1)
        load_w("wo2", wo2)

        nc.scalar.activation(out=warm_out[:], in_=warm_in[:], func=ACT.Abs_reciprocal_sqrt)

        def interleave(name, src, width):
            dst = tile("il_" + name, [P, width * PACK], BF16)
            nc.vector.tensor_copy(
                out=dst[:].rearrange("p (c i j) -> p c j i", i=4, j=PACK),
                in_=src.rearrange("p j (c i) -> p c j i", i=4),
            )
            return dst

        w_il = {k: tile("il_" + k, [P, 256 * PACK], BF16) for k in w_raw}

        def deal(k, copy, part):
            o = w_il[k][:].rearrange("p (e c i j) -> p c j i e", e=2, i=2, j=PACK)
            s = w_raw[k][:].rearrange("p (j c i e) -> p c j i e", j=PACK, i=2, e=2)
            copy(out=o[:, part], in_=s[:, part])

        def interleave_words(b):
            k, n0 = [(0, 0), (0, 128), (1, 0), (2, 0)][b]
            dst = tile("il_h%d" % b, [P, NMM * PACK], BF16)
            words = hh_rows[k][:].bitcast(F32).rearrange("p (h n) -> p h n", h=2)[:, :, n0:n0 + NMM]
            nc.vector.tensor_copy(
                out=dst[:].bitcast(F32).rearrange("p (c i h) -> p c h i", i=2, h=2),
                in_=words.rearrange("p h (c i) -> p c h i", i=2),
            )
            return dst

        def quantize(name, src, width):
            codes = tile("codes_" + name, [P, width], U32)
            scales = tile("scales_" + name, [P, width], U8)
            nc.vector.quantize_mx(out=codes[:].bitcast(FP8X4), scales=scales[:], in_=src[:])
            return codes, scales

        def product(g, bank_of, wq, xq, width):
            rows = slice(R * g, R * (g + 1))
            for e in range(2):
                bank = banks[g][bank_of[e]]
                wc = slice(128 * e, 128 * (e + 1))
                for n0 in range(0, width, NMM):
                    xc = slice(n0, n0 + NMM)
                    nc.tensor.matmul_mx(
                        out=bank[:, e * width + n0:e * width + n0 + NMM],
                        lhsT=wq[0][rows, wc].bitcast(FP8X4), lhsT_scale=wq[1][rows, wc],
                        rhs=xq[0][rows, xc].bitcast(FP8X4), rhs_scale=xq[1][rows, xc],
                        start=True, stop=True,
                    )

        units = [(g, c) for c in range(2) for g in range(G)]
        z1s = {u: tile("z1s%d%d" % u, [P, 2, CHUNK], F32) for u in units}
        prod = {u: tile("prod%d%d" % u, [P, 2, CHUNK], F32) for u in units}
        pieces = [(0, 0, 256), (1, 0, 128), (1, 128, 128)]
        gk = [(g, k) for g in range(G) for k in range(3)]
        sq = {(g, k): tile("sq%d%d" % (g, k), [P, 2, pieces[k][2]], F32) for g, k in gk}
        rs = {(g, k): tile("rs%d%d" % (g, k), [P, 2, pieces[k][2]], F32) for g, k in gk}
        hh = {(g, k): tile("hh%d%d" % (g, k), [P, 2 * pieces[k][2]], BF16) for g, k in gk}
        hh_rows = [tile("hh_rows%d" % k, [P, PACK * pieces[k][2]], BF16) for k in range(3)]
        hs_safe = tile("hs_safe", [P, G, 2], F32)
        inv_hs = tile("inv_hs", [P, G, 2], F32)

        def guard_hs():
            nc.vector.scalar_tensor_tensor(out=hs_safe[:], in0=par["hs"], scalar=0.0, in1=par["hs"],
                                           op0=ALU.is_equal, op1=ALU.add)

        def invert_hs():
            nc.vector.reciprocal(out=inv_hs[:], in_=hs_safe[:])

        def copy_z1(g, c):
            nc.scalar.copy(out=z1s[g, c][:].rearrange("p e n -> p (e n)"), in_=banks[g][2 * c][:])

        z2_banks = [(1, 2), (3, 3)]

        def mul_z(g, c):
            for e in range(2):
                nc.vector.scalar_tensor_tensor(
                    out=prod[g, c][:, e, :], in0=banks[g][z2_banks[c][e]][:, e * CHUNK:(e + 1) * CHUNK],
                    scalar=par["hs"][:, g, e:e + 1], in1=z1s[g, c][:, e, :], op0=ALU.mult, op1=ALU.mult)

        def square_s(g, k):
            c, n0, w = pieces[k]
            for e in range(2):
                nc.scalar.activation(out=sq[g, k][:, e, :], in_=prod[g, c][:, e, n0:n0 + w], func=ACT.Square,
                                     scale=inv_hs[:, g, e:e + 1])

        def square_v(g, k):
            c, n0, w = pieces[k]
            for e in range(2):
                nc.vector.scalar_tensor_tensor(out=sq[g, k][:, e, :], in0=prod[g, c][:, e, n0:n0 + w],
                                               scalar=inv_hs[:, g, e:e + 1], in1=prod[g, c][:, e, n0:n0 + w],
                                               op0=ALU.mult, op1=ALU.mult)

        on_vector = [(1, 0), (0, 2), (1, 2)]

        def root(g, k):
            for e in range(2):
                scale = inv_hs[:, g, e:e + 1] if (g, k) in on_vector else 1.0
                nc.scalar.activation(out=rs[g, k][:, e, :], in_=sq[g, k][:, e, :],
                                     func=ACT.Abs_reciprocal_sqrt, bias=par["so"][:, g, e:e + 1], scale=scale)

        def agree(g, k):
            c, n0, w = pieces[k]
            nc.vector.tensor_tensor(
                out=hh[g, k][:].rearrange("p (c i e) -> p c e i", i=4, e=2),
                in0=prod[g, c][:, :, n0:n0 + w].rearrange("p e (c i) -> p c e i", i=4),
                in1=rs[g, k][:].rearrange("p e (c i) -> p c e i", i=4),
                op=ALU.mult,
            )
            nc.sync.dma_start(
                out=hh_rows[k][R * g:R * (g + 1)].rearrange("p (h w) -> p h w", h=2),
                in_=hh[g, k][:],
            )

        th_tiles = {(g, b): tile("th%d%d" % (g, b), [P, 2, NMM], F32) for g in range(G) for b in range(4)}

        def squash(g, b):
            for e in range(2):
                nc.scalar.activation(out=th_tiles[g, b][:, e, :], in_=banks[g][b][:, e * NMM:(e + 1) * NMM],
                                     func=ACT.Tanh, bias=par["ob"][:, g, e:e + 1])

        def finish(g, b):
            res = tile("res%d%d" % (g, b), [P, 2, NMM], F32)
            for e in range(2):
                nc.vector.tensor_scalar(out=res[:, e, :], in0=th_tiles[g, b][:, e, :],
                                        scalar1=par["osc"][:, g, e:e + 1], scalar2=None, op0=ALU.mult)
            nc.sync.dma_start(out=out[g].rearrange("(q e) n -> q e n", e=2)[:, :, b * NMM:(b + 1) * NMM], in_=res[:])

        def second_layer(b, il):
            hq = quantize("h%d" % b, il, NMM)
            for g in range(G):
                product(g, (b, b), woq, hq, NMM)
            for g in range(G):
                squash(g, b)

        first, rest = slice(0, W_SPLIT), slice(W_SPLIT, 64)
        x0_il = interleave("x0", x_raw[0][:], CHUNK)
        nc.vector.tensor_copy(out=par_dealt[:].rearrange("p (g e i) -> p g e i", g=G, e=2),
                              in_=par_rows[:].rearrange("p (g i e) -> p g e i", g=G, e=2))
        x0q = quantize("x0", x0_il, CHUNK)
        deal("w1", nc.vector.tensor_copy, first)
        deal("w1", nc.scalar.copy, rest)
        nc.vector.transpose(out=par_cols[:], in_=par_dealt[:])
        w1q = quantize("w1", w_il["w1"], 256)
        for g in range(G):
            product(g, (0, 0), w1q, x0q, CHUNK)
        deal("w2", nc.vector.tensor_copy, first)
        deal("w2", nc.scalar.copy, rest)
        guard_hs()
        w2q = quantize("w2", w_il["w2"], 256)
        invert_hs()
        for g in range(G):
            product(g, (1, 2), w2q, x0q, CHUNK)
        copy_z1(0, 0)
        copy_z1(1, 0)
        x1_il = interleave("x1", x_raw[1][:], CHUNK)
        mul_z(0, 0)
        x1q = quantize("x1", x1_il, CHUNK)
        mul_z(1, 0)
        for g in range(G):
            product(g, (2, 2), w1q, x1q, CHUNK)
            product(g, (3, 3), w2q, x1q, CHUNK)
        square_s(0, 0)
        deal("wo2", nc.scalar.copy, slice(WO_SPLIT, 64))
        deal("wo2", nc.vector.tensor_copy, slice(0, WO_SPLIT))
        root(0, 0)
        square_v(1, 0)
        copy_z1(0, 1)
        agree(0, 0)
        root(1, 0)
        mul_z(0, 1)
        copy_z1(1, 1)
        agree(1, 0)
        square_s(0, 1)
        mul_z(1, 1)
        root(0, 1)
        square_v(0, 2)
        square_s(1, 1)
        agree(0, 1)
        square_v(1, 2)
        root(1, 1)
        root(0, 2)
        agree(1, 1)
        root(1, 2)
        agree(0, 2)
        il = interleave_words(0)
        agree(1, 2)
        woq = quantize("wo2", w_il["wo2"], 256)
        second_layer(0, il)
        second_layer(1, interleave_words(1))
        for b in (2, 3):
            il = interleave_words(b)
            finish(0, b - 2)
            second_layer(b, il)
            finish(1, b - 2)
        for b in (2, 3):
            for g in range(G):
                finish(g, b)
